import numpy as np
import ml_dtypes


def mxq(x, axis, fmt="e4m3"):
    dtype, down = {"e4m3": (ml_dtypes.float8_e4m3fn, 7), "e5m2": (ml_dtypes.float8_e5m2, 14)}[fmt]
    v = np.moveaxis(np.asarray(x, np.float32).astype(ml_dtypes.bfloat16).astype(np.float64), axis, -1)
    blocks = v.reshape(v.shape[:-1] + (-1, 32))
    amax = np.abs(blocks).max(-1, keepdims=True)
    byte = np.maximum(np.where(amax > 0, np.frexp(amax)[1] - 1 + 127, 0) - down, 1)
    scale = np.exp2(byte - 127.0)
    codes = (blocks / scale).astype(np.float32).astype(dtype).astype(np.float64)
    return np.moveaxis((codes * scale).reshape(v.shape), -1, axis)


WIDE = False


def mx_kscale(k, group=512):
    if not WIDE:
        return np.ones(k)
    levels = np.array([10, -10, 5, -5, 0])
    if group != 512:
        return np.exp2(np.random.permutation(np.resize(levels, k // group))).repeat(group)
    if k % 512:
        return np.exp2(np.random.permutation(np.resize(levels, k // 32))).repeat(32)
    a = np.empty((k // 512, 16))
    for p in range(k // 512):
        a[p, :8] = np.random.permutation(np.resize(levels, 8))
        for g in range(8):
            far = levels[np.abs(levels - a[p, g]) >= 10]
            a[p, g + 8] = far[np.random.randint(len(far))]
    return np.exp2(a.ravel()).repeat(32)


def f64(x):
    return np.asarray(x).astype(np.float64)


E2M1 = np.array([0.0, 0.5, 1.0, 1.5, 2.0, 3.0, 4.0, 6.0, -0.0, -0.5, -1.0, -1.5, -2.0, -3.0, -4.0, -6.0])


def pack_group(w):
    k, n = w.shape
    w = f64(np.asarray(w, np.float32).astype(ml_dtypes.bfloat16)).reshape(k // 32, 32, n)
    amax = np.abs(w).max(1)
    mant, ex = np.frexp(amax / 6.0)
    byte = np.clip(np.where(amax > 0, np.where(mant > 0.5, ex, ex - 1) + 127, 1), 1, 254)
    scaled = (w * np.exp2(127.0 - byte)[:, None, :]).reshape(k, n).astype(np.float32)
    c = np.ascontiguousarray(scaled.reshape(k // 4, 4, n).transpose(0, 2, 1)).astype(ml_dtypes.float4_e2m1fn).view(np.uint8) & 0xF
    return np.ascontiguousarray((c[..., 0::2] | (c[..., 1::2] << 4)).reshape(k // 4, 2 * n)), byte.astype(np.uint8)


def unpack_group(words, scales):
    p, n = words.shape[0], scales.shape[1]
    words = np.ascontiguousarray(words).reshape(p, n, 2)
    nib = np.empty((p, n, 4), np.uint8)
    nib[..., 0::2] = words & 0xF
    nib[..., 1::2] = words >> 4
    return E2M1[nib].transpose(0, 2, 1).reshape(4 * p, n) * np.repeat(np.exp2(scales.astype(np.float64) - 127.0), 32, axis=0)


G, D, M, N = 2, 256, 256, 1024


def setup_inputs():
    n = np.random.standard_normal
    s = mx_kscale(D, 0)[:, None]
    w_ = [pack_group(w) for w in n((G, D, M)) / np.sqrt(D) / s]
    return {
        "x": (n((G, D, N)) * s).astype(np.float32),
        "w_words": np.stack([w[0] for w in w_]),
        "w_scales": np.stack([w[1] for w in w_]),
        "b": (0.5 * n((G, M, 1))).astype(np.float32),
        "r": n((G, M, N)).astype(np.float32),
    }


def reference(x, w_words, w_scales, b, r):
    xq = mxq(f64(x), 1, "e4m3")
    y = np.stack([unpack_group(w_words[g], w_scales[g]) for g in range(G)]).transpose(0, 2, 1) @ xq
    y = y + f64(b)
    y = np.maximum(y, 0.0)
    y = y + f64(r)
    return y

@@ -1,0 +1,150 @@
+from contextlib import ExitStack
+
+import concourse.mybir as mybir
+
+G, D, M, N = 2, 256, 256, 1024
+FLOPS = 2 * G * D * M * N
+
+F32 = mybir.dt.float32
+BF16 = mybir.dt.bfloat16
+I32 = mybir.dt.int32
+U32 = mybir.dt.uint32
+U8 = mybir.dt.uint8
+FP8X4 = mybir.dt.float8_e4m3fn_x4
+FP4X4 = mybir.dt.float4_e2m1fn_x4
+ACT = mybir.ActivationFunctionType
+ALU = mybir.AluOpType
+
+P = 128
+PACK = 4
+ROWS = D // PACK
+M_TILE = 128
+M_TILES = M // M_TILE
+N_TILE = 512
+HALVES = N // N_TILE
+QUANT_COLS = 256
+SCALAR_COLS = (192, 128)
+BIAS_PITCH = 8
+
+
+def tile_rows_glin_relu_bias_res_kernel(tc, x, w_words, w_scales, b, r, out):
+    nc = tc.nc
+
+    x_rows = x.rearrange("g (p j) n -> (g p) j n", j=PACK)
+    out_rows = out.rearrange("g (t p) n -> t p g n", p=P)
+    scale_rows = w_scales.rearrange("g f m -> (g f) m").bitcast(I32)
+
+    with ExitStack() as ctx:
+        sb = ctx.enter_context(tc.tile_pool(name="sb", bufs=1))
+        ps = ctx.enter_context(tc.psum_pool(name="ps", bufs=1))
+        ctx.enter_context(tc.manual_schedule())
+
+        w_sb = sb.tile([P, 2 * M], U8, name="w_sb", align_bytes=64)
+        ws_sb = sb.tile([P, M], U8, name="ws_sb", align_bytes=64)
+        bias = sb.tile([P, G * M_TILES, BIAS_PITCH], F32, name="bias")
+        raw = [sb.tile([P, PACK, N_TILE], F32, name="raw%d" % h, align_bytes=64) for h in range(HALVES)]
+        grouped = [sb.tile([P, N_TILE, PACK], BF16, name="grouped%d" % h, align_bytes=64) for h in range(HALVES)]
+        codes = [sb.tile([P, N_TILE], U32, name="codes%d" % h, align_bytes=64) for h in range(HALVES)]
+        scales = [sb.tile([P, N_TILE], U8, name="scales%d" % h, align_bytes=64) for h in range(HALVES)]
+        res = [sb.tile([P, G, N], F32, name="res%d" % t, align_bytes=64) for t in range(M_TILES)]
+        y = [sb.tile([P, G, N], F32, name="y%d" % t, align_bytes=64) for t in range(M_TILES)]
+        acc = {}
+        for g in range(G):
+            for t in range(M_TILES):
+                for h in range(HALVES):
+                    acc[g, t, h] = ps.tile([M_TILE, N_TILE], F32, name="acc%d%d%d" % (g, t, h))
+
+        def cols(h):
+            return slice(h * N_TILE, (h + 1) * N_TILE)
+
+        def load_x(h):
+            nc.sync.dma_start(out=raw[h][:], in_=x_rows[:, :, cols(h)])
+
+        def load_weights():
+            nc.sync.dma_start(out=w_sb[:].bitcast(I32), in_=w_words.rearrange("g p c -> (g p) c").bitcast(I32))
+            for q in range(4):
+                nc.sync.dma_start(out=ws_sb[32 * q : 32 * q + 4, :].bitcast(I32), in_=scale_rows[4 * q : 4 * q + 4, :])
+
+        def load_bias():
+            with nc.allow_non_contiguous_dma(reason="one bias value for each partition"):
+                nc.sync.dma_start(out=bias[:, :, 0:1], in_=b.rearrange("g (t p) o -> p (g t) o", p=P))
+
+        def load_res(g, t):
+            nc.sync.dma_start(out=res[t][:, g, :], in_=r[g, t * P : (t + 1) * P, :])
+
+        def views(h, lo, hi):
+            dst = grouped[h][:, lo:hi, :].rearrange("p (c i) j -> p c j i", i=4)
+            src = raw[h][:, :, lo:hi].rearrange("p j (c i) -> p c j i", i=4)
+            return dst, src
+
+        def interleave_vector(h, lo, hi):
+            dst, src = views(h, lo, hi)
+            nc.vector.tensor_copy(out=dst, in_=src)
+
+        def interleave_scalar(h, lo, hi):
+            dst, src = views(h, lo, hi)
+            nc.scalar.copy(out=dst, in_=src)
+
+        def quantize(h, lo):
+            hi = lo + QUANT_COLS
+            nc.vector.quantize_mx(
+                out=codes[h][:, lo:hi].bitcast(FP8X4),
+                scales=scales[h][:, lo:hi],
+                in_=grouped[h][:, lo:hi, :].rearrange("p c j -> p (c j)"),
+            )
+
+        def prepare_vector(h):
+            interleave_vector(h, 0, QUANT_COLS)
+            interleave_vector(h, QUANT_COLS, N_TILE - SCALAR_COLS[h])
+            quantize(h, 0)
+            quantize(h, QUANT_COLS)
+
+        def multiply(g, t, h):
+            rows = slice(g * ROWS, (g + 1) * ROWS)
+            nc.tensor.matmul_mx(
+                out=acc[g, t, h][:],
+                lhsT=w_sb[rows, 2 * t * M_TILE : 2 * (t + 1) * M_TILE].bitcast(FP4X4),
+                lhsT_scale=ws_sb[rows, t * M_TILE : (t + 1) * M_TILE],
+                rhs=codes[h][rows, :].bitcast(FP8X4),
+                rhs_scale=scales[h][rows, :],
+                start=True,
+                stop=True,
+            )
+
+        def relu(g, t, h):
+            k = g * M_TILES + t
+            nc.scalar.activation(out=y[t][:, g, cols(h)], in_=acc[g, t, h][:], func=ACT.Relu, bias=bias[:, k, 0:1])
+
+        def add(g, t, h):
+            nc.vector.tensor_tensor(out=y[t][:, g, cols(h)], in0=y[t][:, g, cols(h)], in1=res[t][:, g, cols(h)], op=ALU.add)
+
+        nc.vector.memset(ws_sb[:].bitcast(I32), 0)
+        load_x(0)
+        load_weights()
+        load_x(1)
+        load_bias()
+        for t in range(M_TILES):
+            for g in range(G):
+                load_res(g, t)
+
+        interleave_scalar(0, N_TILE - SCALAR_COLS[0], N_TILE)
+        prepare_vector(0)
+        for t in range(M_TILES):
+            for g in range(G):
+                multiply(g, t, 0)
+        interleave_scalar(1, N_TILE - SCALAR_COLS[1], N_TILE)
+        prepare_vector(1)
+        for t in range(M_TILES):
+            for g in range(G):
+                multiply(g, t, 1)
+
+        for g, t, h in ((0, 0, 0), (1, 0, 0), (0, 1, 0), (0, 0, 1), (1, 0, 1), (0, 1, 1), (1, 1, 0), (1, 1, 1)):
+            relu(g, t, h)
+        for h in range(HALVES):
+            for g in range(G):
+                add(g, 0, h)
+            nc.sync.dma_start(out=out_rows[0][:, :, cols(h)], in_=y[0][:, :, cols(h)])
+        for g in range(G):
+            for h in range(HALVES):
+                add(g, 1, h)
+            nc.sync.dma_start(out=out_rows[1][:, g, :], in_=y[1][:, g, :])

@@ -23,8 +23,8 @@ M_TILES = M // M_TILE
 N_TILE = 512
 HALVES = N // N_TILE
 QUANT_COLS = 256
-SCALAR_COLS = (192, 128)
-BIAS_PITCH = 8
+X_CHUNKS = ((0, 512), (512, 768), (768, 1024))
+SCALAR_COLS = 192
 
 
 def tile_rows_glin_relu_bias_res_kernel(tc, x, w_words, w_scales, b, r, out):
@@ -32,6 +32,7 @@ def tile_rows_glin_relu_bias_res_kernel(tc, x, w_words, w_scales, b, r, out):
 
     x_rows = x.rearrange("g (p j) n -> (g p) j n", j=PACK)
     out_rows = out.rearrange("g (t p) n -> t p g n", p=P)
+    r_rows = r.rearrange("g (t p) n -> t p g n", p=P)
     scale_rows = w_scales.rearrange("g f m -> (g f) m").bitcast(I32)
 
     with ExitStack() as ctx:
@@ -41,13 +42,18 @@ def tile_rows_glin_relu_bias_res_kernel(tc, x, w_words, w_scales, b, r, out):
 
         w_sb = sb.tile([P, 2 * M], U8, name="w_sb", align_bytes=64)
         ws_sb = sb.tile([P, M], U8, name="ws_sb", align_bytes=64)
-        bias = sb.tile([P, G * M_TILES, BIAS_PITCH], F32, name="bias")
-        raw = [sb.tile([P, PACK, N_TILE], F32, name="raw%d" % h, align_bytes=64) for h in range(HALVES)]
+        bias_rows = sb.tile([P, P], F32, name="bias_rows", align_bytes=64)
+        bias = sb.tile([P, P], F32, name="bias", align_bytes=64)
+        raw = [sb.tile([P, PACK, hi - lo], F32, name="raw%d" % lo, align_bytes=64) for lo, hi in X_CHUNKS]
         grouped = [sb.tile([P, N_TILE, PACK], BF16, name="grouped%d" % h, align_bytes=64) for h in range(HALVES)]
         codes = [sb.tile([P, N_TILE], U32, name="codes%d" % h, align_bytes=64) for h in range(HALVES)]
         scales = [sb.tile([P, N_TILE], U8, name="scales%d" % h, align_bytes=64) for h in range(HALVES)]
-        res = [sb.tile([P, G, N], F32, name="res%d" % t, align_bytes=64) for t in range(M_TILES)]
-        y = [sb.tile([P, G, N], F32, name="y%d" % t, align_bytes=64) for t in range(M_TILES)]
+        res = {}
+        y = {}
+        for t in range(M_TILES):
+            for h in range(HALVES):
+                res[t, h] = sb.tile([P, G, N_TILE], F32, name="res%d%d" % (t, h), align_bytes=64)
+                y[t, h] = sb.tile([P, G, N_TILE], F32, name="y%d%d" % (t, h), align_bytes=64)
         acc = {}
         for g in range(G):
             for t in range(M_TILES):
@@ -57,47 +63,53 @@ def tile_rows_glin_relu_bias_res_kernel(tc, x, w_words, w_scales, b, r, out):
         def cols(h):
             return slice(h * N_TILE, (h + 1) * N_TILE)
 
-        def load_x(h):
-            nc.sync.dma_start(out=raw[h][:], in_=x_rows[:, :, cols(h)])
+        def load_x(c):
+            lo, hi = X_CHUNKS[c]
+            nc.sync.dma_start(out=raw[c][:], in_=x_rows[:, :, lo:hi])
 
         def load_weights():
             nc.sync.dma_start(out=w_sb[:].bitcast(I32), in_=w_words.rearrange("g p c -> (g p) c").bitcast(I32))
+
+        def load_scales():
             for q in range(4):
                 nc.sync.dma_start(out=ws_sb[32 * q : 32 * q + 4, :].bitcast(I32), in_=scale_rows[4 * q : 4 * q + 4, :])
 
         def load_bias():
-            with nc.allow_non_contiguous_dma(reason="one bias value for each partition"):
-                nc.sync.dma_start(out=bias[:, :, 0:1], in_=b.rearrange("g (t p) o -> p (g t) o", p=P))
-
-        def load_res(g, t):
-            nc.sync.dma_start(out=res[t][:, g, :], in_=r[g, t * P : (t + 1) * P, :])
-
-        def views(h, lo, hi):
-            dst = grouped[h][:, lo:hi, :].rearrange("p (c i) j -> p c j i", i=4)
-            src = raw[h][:, :, lo:hi].rearrange("p j (c i) -> p c j i", i=4)
-            return dst, src
-
-        def interleave_vector(h, lo, hi):
-            dst, src = views(h, lo, hi)
-            nc.vector.tensor_copy(out=dst, in_=src)
-
-        def interleave_scalar(h, lo, hi):
-            dst, src = views(h, lo, hi)
-            nc.scalar.copy(out=dst, in_=src)
-
-        def quantize(h, lo):
-            hi = lo + QUANT_COLS
-            nc.vector.quantize_mx(
-                out=codes[h][:, lo:hi].bitcast(FP8X4),
-                scales=scales[h][:, lo:hi],
-                in_=grouped[h][:, lo:hi, :].rearrange("p c j -> p (c j)"),
+            nc.sync.dma_start(
+                out=bias_rows[0:P:32, :].rearrange("q (k j) -> q k j", j=32),
+                in_=b.rearrange("g (t q j) o -> q (g t) (j o)", q=4, j=32),
             )
 
-        def prepare_vector(h):
-            interleave_vector(h, 0, QUANT_COLS)
-            interleave_vector(h, QUANT_COLS, N_TILE - SCALAR_COLS[h])
-            quantize(h, 0)
-            quantize(h, QUANT_COLS)
+        def load_res(t, h):
+            nc.sync.dma_start(out=res[t, h][:], in_=r_rows[t][:, :, cols(h)])
+
+        def store(t, h):
+            nc.sync.dma_start(out=out_rows[t][:, :, cols(h)], in_=y[t, h][:])
+
+        def views(lo, hi):
+            c = max(i for i in range(len(X_CHUNKS)) if X_CHUNKS[i][0] <= lo)
+            first = X_CHUNKS[c][0]
+            h, at = divmod(lo, N_TILE)
+            dst = grouped[h][:, at : at + hi - lo, :].rearrange("p (c i) j -> p c j i", i=4)
+            src = raw[c][:, :, lo - first : hi - first].rearrange("p j (c i) -> p c j i", i=4)
+            return dst, src
+
+        def interleave_vector(lo, hi):
+            dst, src = views(lo, hi)
+            nc.vector.tensor_copy(out=dst, in_=src)
+
+        def interleave_scalar(lo, hi):
+            dst, src = views(lo, hi)
+            nc.scalar.copy(out=dst, in_=src)
+
+        def quantize(lo, hi):
+            h, at = divmod(lo, N_TILE)
+            part = slice(at, at + hi - lo)
+            nc.vector.quantize_mx(
+                out=codes[h][:, part].bitcast(FP8X4),
+                scales=scales[h][:, part],
+                in_=grouped[h][:, part, :].rearrange("p c j -> p (c j)"),
+            )
 
         def multiply(g, t, h):
             rows = slice(g * ROWS, (g + 1) * ROWS)
@@ -113,38 +125,44 @@ def tile_rows_glin_relu_bias_res_kernel(tc, x, w_words, w_scales, b, r, out):
 
         def relu(g, t, h):
             k = g * M_TILES + t
-            nc.scalar.activation(out=y[t][:, g, cols(h)], in_=acc[g, t, h][:], func=ACT.Relu, bias=bias[:, k, 0:1])
+            nc.scalar.activation(out=y[t, h][:, g, :], in_=acc[g, t, h][:], func=ACT.Relu, bias=bias[:, 32 * k : 32 * k + 1])
 
         def add(g, t, h):
-            nc.vector.tensor_tensor(out=y[t][:, g, cols(h)], in0=y[t][:, g, cols(h)], in1=res[t][:, g, cols(h)], op=ALU.add)
+            nc.vector.tensor_tensor(out=y[t, h][:, g, :], in0=y[t, h][:, g, :], in1=res[t, h][:, g, :], op=ALU.add)
 
         nc.vector.memset(ws_sb[:].bitcast(I32), 0)
-        load_x(0)
+        nc.vector.memset(bias_rows[:], 0.0)
         load_weights()
-        load_x(1)
+        load_x(0)
+        load_scales()
         load_bias()
-        for t in range(M_TILES):
-            for g in range(G):
-                load_res(g, t)
+        load_x(1)
+        load_x(2)
+        for h in range(HALVES):
+            for t in range(M_TILES):
+                load_res(t, h)
 
-        interleave_scalar(0, N_TILE - SCALAR_COLS[0], N_TILE)
-        prepare_vector(0)
+        interleave_scalar(N_TILE - SCALAR_COLS, N_TILE)
+        interleave_vector(0, 256)
+        interleave_vector(256, N_TILE - SCALAR_COLS)
+        quantize(0, 256)
+        quantize(256, 512)
+        nc.vector.transpose(out=bias[:], in_=bias_rows[:])
         for t in range(M_TILES):
             for g in range(G):
                 multiply(g, t, 0)
-        interleave_scalar(1, N_TILE - SCALAR_COLS[1], N_TILE)
-        prepare_vector(1)
+        for lo in (512, 768):
+            interleave_vector(lo, lo + 128)
+            interleave_vector(lo + 128, lo + 256)
+            quantize(lo, lo + 128)
+            quantize(lo + 128, lo + 256)
         for t in range(M_TILES):
             for g in range(G):
                 multiply(g, t, 1)
 
-        for g, t, h in ((0, 0, 0), (1, 0, 0), (0, 1, 0), (0, 0, 1), (1, 0, 1), (0, 1, 1), (1, 1, 0), (1, 1, 1)):
-            relu(g, t, h)
         for h in range(HALVES):
-            for g in range(G):
-                add(g, 0, h)
-            nc.sync.dma_start(out=out_rows[0][:, :, cols(h)], in_=y[0][:, :, cols(h)])
-        for g in range(G):
-            for h in range(HALVES):
-                add(g, 1, h)
-            nc.sync.dma_start(out=out_rows[1][:, g, :], in_=y[1][:, g, :])
+            for t in range(M_TILES):
+                for g in range(G):
+                    relu(g, t, h)
+                    add(g, t, h)
+                store(t, h)

@@ -23,16 +23,14 @@ M_TILES = M // M_TILE
 N_TILE = 512
 HALVES = N // N_TILE
 QUANT_COLS = 256
-X_CHUNKS = ((0, 512), (512, 768), (768, 1024))
-SCALAR_COLS = 192
+X_CHUNKS = ((0, 512), (512, 1024))
+SCALAR_COLS = (192, 128)
 
 
 def tile_rows_glin_relu_bias_res_kernel(tc, x, w_words, w_scales, b, r, out):
     nc = tc.nc
 
     x_rows = x.rearrange("g (p j) n -> (g p) j n", j=PACK)
-    out_rows = out.rearrange("g (t p) n -> t p g n", p=P)
-    r_rows = r.rearrange("g (t p) n -> t p g n", p=P)
     scale_rows = w_scales.rearrange("g f m -> (g f) m").bitcast(I32)
 
     with ExitStack() as ctx:
@@ -51,9 +49,9 @@ def tile_rows_glin_relu_bias_res_kernel(tc, x, w_words, w_scales, b, r, out):
         res = {}
         y = {}
         for t in range(M_TILES):
-            for h in range(HALVES):
-                res[t, h] = sb.tile([P, G, N_TILE], F32, name="res%d%d" % (t, h), align_bytes=64)
-                y[t, h] = sb.tile([P, G, N_TILE], F32, name="y%d%d" % (t, h), align_bytes=64)
+            for g in range(G):
+                res[g, t] = sb.tile([P, N], F32, name="res%d%d" % (g, t), align_bytes=64)
+                y[g, t] = sb.tile([P, N], F32, name="y%d%d" % (g, t), align_bytes=64)
         acc = {}
         for g in range(G):
             for t in range(M_TILES):
@@ -80,11 +78,11 @@ def tile_rows_glin_relu_bias_res_kernel(tc, x, w_words, w_scales, b, r, out):
                 in_=b.rearrange("g (t q j) o -> q (g t) (j o)", q=4, j=32),
             )
 
-        def load_res(t, h):
-            nc.sync.dma_start(out=res[t, h][:], in_=r_rows[t][:, :, cols(h)])
+        def load_res(g, t):
+            nc.sync.dma_start(out=res[g, t][:], in_=r[g, t * P : (t + 1) * P, :])
 
-        def store(t, h):
-            nc.sync.dma_start(out=out_rows[t][:, :, cols(h)], in_=y[t, h][:])
+        def store(g, t):
+            nc.sync.dma_start(out=out[g, t * P : (t + 1) * P, :], in_=y[g, t][:])
 
         def views(lo, hi):
             c = max(i for i in range(len(X_CHUNKS)) if X_CHUNKS[i][0] <= lo)
@@ -125,10 +123,10 @@ def tile_rows_glin_relu_bias_res_kernel(tc, x, w_words, w_scales, b, r, out):
 
         def relu(g, t, h):
             k = g * M_TILES + t
-            nc.scalar.activation(out=y[t, h][:, g, :], in_=acc[g, t, h][:], func=ACT.Relu, bias=bias[:, 32 * k : 32 * k + 1])
+            nc.scalar.activation(out=y[g, t][:, cols(h)], in_=acc[g, t, h][:], func=ACT.Relu, bias=bias[:, 32 * k : 32 * k + 1])
 
         def add(g, t, h):
-            nc.vector.tensor_tensor(out=y[t, h][:, g, :], in0=y[t, h][:, g, :], in1=res[t, h][:, g, :], op=ALU.add)
+            nc.vector.tensor_tensor(out=y[g, t][:, cols(h)], in0=y[g, t][:, cols(h)], in1=res[g, t][:, cols(h)], op=ALU.add)
 
         nc.vector.memset(ws_sb[:].bitcast(I32), 0)
         nc.vector.memset(bias_rows[:], 0.0)
@@ -137,32 +135,25 @@ def tile_rows_glin_relu_bias_res_kernel(tc, x, w_words, w_scales, b, r, out):
         load_scales()
         load_bias()
         load_x(1)
-        load_x(2)
+        for t in range(M_TILES):
+            for g in range(G):
+                load_res(g, t)
+
         for h in range(HALVES):
-            for t in range(M_TILES):
-                load_res(t, h)
-
-        interleave_scalar(N_TILE - SCALAR_COLS, N_TILE)
-        interleave_vector(0, 256)
-        interleave_vector(256, N_TILE - SCALAR_COLS)
-        quantize(0, 256)
-        quantize(256, 512)
-        nc.vector.transpose(out=bias[:], in_=bias_rows[:])
-        for t in range(M_TILES):
-            for g in range(G):
-                multiply(g, t, 0)
-        for lo in (512, 768):
-            interleave_vector(lo, lo + 128)
-            interleave_vector(lo + 128, lo + 256)
-            quantize(lo, lo + 128)
-            quantize(lo + 128, lo + 256)
-        for t in range(M_TILES):
-            for g in range(G):
-                multiply(g, t, 1)
-
+            lo = h * N_TILE
+            interleave_scalar(lo + N_TILE - SCALAR_COLS[h], lo + N_TILE)
+            interleave_vector(lo, lo + 256)
+            interleave_vector(lo + 256, lo + N_TILE - SCALAR_COLS[h])
+            quantize(lo, lo + 256)
+            quantize(lo + 256, lo + 512)
+            if h == 0:
+                nc.vector.transpose(out=bias[:], in_=bias_rows[:])
         for h in range(HALVES):
             for t in range(M_TILES):
                 for g in range(G):
-                    relu(g, t, h)
-                    add(g, t, h)
-                store(t, h)
+                    multiply(g, t, h)
+
+        for g, t, h in ((0, 0, 0), (1, 0, 0), (0, 1, 0), (0, 0, 1), (1, 1, 0), (1, 0, 1), (0, 1, 1), (1, 1, 1)):
+            relu(g, t, h)
+            add(g, t, h)
+            nc.sync.dma_start(out=out[g, t * P : (t + 1) * P, cols(h)], in_=y[g, t][:, cols(h)])

@@ -23,14 +23,13 @@ M_TILES = M // M_TILE
 N_TILE = 512
 HALVES = N // N_TILE
 QUANT_COLS = 256
-X_CHUNKS = ((0, 512), (512, 1024))
-SCALAR_COLS = (192, 128)
+SCALAR_COLS = (192, 192)
 
 
 def tile_rows_glin_relu_bias_res_kernel(tc, x, w_words, w_scales, b, r, out):
     nc = tc.nc
 
-    x_rows = x.rearrange("g (p j) n -> (g p) j n", j=PACK)
+    x_pairs = x.rearrange("g (p a e) n -> (g p) a (e n)", a=2, e=2)
     scale_rows = w_scales.rearrange("g f m -> (g f) m").bitcast(I32)
 
     with ExitStack() as ctx:
@@ -42,7 +41,10 @@ def tile_rows_glin_relu_bias_res_kernel(tc, x, w_words, w_scales, b, r, out):
         ws_sb = sb.tile([P, M], U8, name="ws_sb", align_bytes=64)
         bias_rows = sb.tile([P, P], F32, name="bias_rows", align_bytes=64)
         bias = sb.tile([P, P], F32, name="bias", align_bytes=64)
-        raw = [sb.tile([P, PACK, hi - lo], F32, name="raw%d" % lo, align_bytes=64) for lo, hi in X_CHUNKS]
+        raw = sb.tile([P, 12, N_TILE], F32, name="raw", align_bytes=64)
+        early = raw[:, 0:6, :].rearrange("p (a s) n -> p a s n", a=2)
+        spaced = raw[:].rearrange("p (e a s) n -> p a e s n", e=2, a=2)
+        rows_of = [early[:, :, 0:3:2, :], spaced[:, :, :, 1, :]]
         grouped = [sb.tile([P, N_TILE, PACK], BF16, name="grouped%d" % h, align_bytes=64) for h in range(HALVES)]
         codes = [sb.tile([P, N_TILE], U32, name="codes%d" % h, align_bytes=64) for h in range(HALVES)]
         scales = [sb.tile([P, N_TILE], U8, name="scales%d" % h, align_bytes=64) for h in range(HALVES)]
@@ -61,9 +63,11 @@ def tile_rows_glin_relu_bias_res_kernel(tc, x, w_words, w_scales, b, r, out):
         def cols(h):
             return slice(h * N_TILE, (h + 1) * N_TILE)
 
-        def load_x(c):
-            lo, hi = X_CHUNKS[c]
-            nc.sync.dma_start(out=raw[c][:], in_=x_rows[:, :, lo:hi])
+        def load_x_early():
+            nc.sync.dma_start(out=early.rearrange("p a s n -> p a (s n)"), in_=x_pairs[:, :, 0 : N + N_TILE])
+
+        def load_x_late():
+            nc.sync.dma_start(out=spaced[:, :, 1, 1, :], in_=x_pairs[:, :, N + N_TILE : 2 * N])
 
         def load_weights():
             nc.sync.dma_start(out=w_sb[:].bitcast(I32), in_=w_words.rearrange("g p c -> (g p) c").bitcast(I32))
@@ -78,18 +82,16 @@ def tile_rows_glin_relu_bias_res_kernel(tc, x, w_words, w_scales, b, r, out):
                 in_=b.rearrange("g (t q j) o -> q (g t) (j o)", q=4, j=32),
             )
 
-        def load_res(g, t):
-            nc.sync.dma_start(out=res[g, t][:], in_=r[g, t * P : (t + 1) * P, :])
+        def load_res(g, t, lo, hi):
+            nc.sync.dma_start(out=res[g, t][:, lo:hi], in_=r[g, t * P : (t + 1) * P, lo:hi])
 
         def store(g, t):
             nc.sync.dma_start(out=out[g, t * P : (t + 1) * P, :], in_=y[g, t][:])
 
         def views(lo, hi):
-            c = max(i for i in range(len(X_CHUNKS)) if X_CHUNKS[i][0] <= lo)
-            first = X_CHUNKS[c][0]
             h, at = divmod(lo, N_TILE)
-            dst = grouped[h][:, at : at + hi - lo, :].rearrange("p (c i) j -> p c j i", i=4)
-            src = raw[c][:, :, lo - first : hi - first].rearrange("p j (c i) -> p c j i", i=4)
+            dst = grouped[h][:, at : at + hi - lo, :].rearrange("p (c i) (a e) -> p c a e i", i=4, e=2)
+            src = rows_of[h][:, :, :, at : at + hi - lo].rearrange("p a e (c i) -> p c a e i", i=4)
             return dst, src
 
         def interleave_vector(lo, hi):
@@ -131,13 +133,15 @@ def tile_rows_glin_relu_bias_res_kernel(tc, x, w_words, w_scales, b, r, out):
         nc.vector.memset(ws_sb[:].bitcast(I32), 0)
         nc.vector.memset(bias_rows[:], 0.0)
         load_weights()
-        load_x(0)
+        load_x_early()
         load_scales()
         load_bias()
-        load_x(1)
-        for t in range(M_TILES):
-            for g in range(G):
-                load_res(g, t)
+        load_x_late()
+        load_res(0, 0, 0, N)
+        load_res(1, 0, 0, N_TILE)
+        load_res(0, 1, 0, N)
+        load_res(1, 1, 0, N)
+        load_res(1, 0, N_TILE, N)
 
         for h in range(HALVES):
             lo = h * N_TILE
@@ -148,12 +152,10 @@ def tile_rows_glin_relu_bias_res_kernel(tc, x, w_words, w_scales, b, r, out):
             quantize(lo + 256, lo + 512)
             if h == 0:
                 nc.vector.transpose(out=bias[:], in_=bias_rows[:])
-        for h in range(HALVES):
-            for t in range(M_TILES):
-                for g in range(G):
-                    multiply(g, t, h)
+        for g, t, h in ((0, 0, 0), (1, 0, 0), (0, 1, 0), (0, 0, 1), (1, 1, 0), (0, 1, 1), (1, 1, 1), (1, 0, 1)):
+            multiply(g, t, h)
 
-        for g, t, h in ((0, 0, 0), (1, 0, 0), (0, 1, 0), (0, 0, 1), (1, 1, 0), (1, 0, 1), (0, 1, 1), (1, 1, 1)):
+        for g, t, h in ((0, 0, 0), (1, 0, 0), (0, 1, 0), (0, 0, 1), (1, 1, 0), (0, 1, 1), (1, 1, 1), (1, 0, 1)):
             relu(g, t, h)
             add(g, t, h)
             nc.sync.dma_start(out=out[g, t * P : (t + 1) * P, cols(h)], in_=y[g, t][:, cols(h)])

from contextlib import ExitStack

import concourse.mybir as mybir

G, D, M, N = 2, 256, 256, 1024
FLOPS = 2 * G * D * M * N

F32 = mybir.dt.float32
BF16 = mybir.dt.bfloat16
I32 = mybir.dt.int32
U32 = mybir.dt.uint32
U8 = mybir.dt.uint8
FP8X4 = mybir.dt.float8_e4m3fn_x4
FP4X4 = mybir.dt.float4_e2m1fn_x4
ACT = mybir.ActivationFunctionType
ALU = mybir.AluOpType

P = 128
PACK = 4
ROWS = D // PACK
M_TILE = 128
M_TILES = M // M_TILE
N_TILE = 512
HALVES = N // N_TILE
QUANT_COLS = 256
SCALAR_COLS = (192, 192)


def tile_rows_glin_relu_bias_res_kernel(tc, x, w_words, w_scales, b, r, out):
    nc = tc.nc

    x_pairs = x.rearrange("g (p a e) n -> (g p) a (e n)", a=2, e=2)
    scale_rows = w_scales.rearrange("g f m -> (g f) m").bitcast(I32)

    with ExitStack() as ctx:
        sb = ctx.enter_context(tc.tile_pool(name="sb", bufs=1))
        ps = ctx.enter_context(tc.psum_pool(name="ps", bufs=1))
        ctx.enter_context(tc.manual_schedule())

        w_sb = sb.tile([P, 2 * M], U8, name="w_sb", align_bytes=64)
        ws_sb = sb.tile([P, M], U8, name="ws_sb", align_bytes=64)
        bias_rows = sb.tile([P, P], F32, name="bias_rows", align_bytes=64)
        bias = sb.tile([P, P], F32, name="bias", align_bytes=64)
        raw = sb.tile([P, 12, N_TILE], F32, name="raw", align_bytes=64)
        early = raw[:, 0:6, :].rearrange("p (a s) n -> p a s n", a=2)
        spaced = raw[:].rearrange("p (e a s) n -> p a e s n", e=2, a=2)
        rows_of = [early[:, :, 0:3:2, :], spaced[:, :, :, 1, :]]
        grouped = [sb.tile([P, N_TILE, PACK], BF16, name="grouped%d" % h, align_bytes=64) for h in range(HALVES)]
        codes = [sb.tile([P, N_TILE], U32, name="codes%d" % h, align_bytes=64) for h in range(HALVES)]
        scales = [sb.tile([P, N_TILE], U8, name="scales%d" % h, align_bytes=64) for h in range(HALVES)]
        res = {}
        y = {}
        for t in range(M_TILES):
            for g in range(G):
                res[g, t] = sb.tile([P, N], F32, name="res%d%d" % (g, t), align_bytes=64)
                y[g, t] = sb.tile([P, N], F32, name="y%d%d" % (g, t), align_bytes=64)
        acc = {}
        for g in range(G):
            for t in range(M_TILES):
                for h in range(HALVES):
                    acc[g, t, h] = ps.tile([M_TILE, N_TILE], F32, name="acc%d%d%d" % (g, t, h))

        def cols(h):
            return slice(h * N_TILE, (h + 1) * N_TILE)

        def load_x_early():
            nc.sync.dma_start(out=early.rearrange("p a s n -> p a (s n)"), in_=x_pairs[:, :, 0 : N + N_TILE])

        def load_x_late():
            nc.sync.dma_start(out=spaced[:, :, 1, 1, :], in_=x_pairs[:, :, N + N_TILE : 2 * N])

        def load_weights():
            nc.sync.dma_start(out=w_sb[:].bitcast(I32), in_=w_words.rearrange("g p c -> (g p) c").bitcast(I32))

        def load_scales():
            for q in range(4):
                nc.sync.dma_start(out=ws_sb[32 * q : 32 * q + 4, :].bitcast(I32), in_=scale_rows[4 * q : 4 * q + 4, :])

        def load_bias():
            nc.sync.dma_start(
                out=bias_rows[0:P:32, :].rearrange("q (k j) -> q k j", j=32),
                in_=b.rearrange("g (t q j) o -> q (g t) (j o)", q=4, j=32),
            )

        def load_res(g, t, lo, hi):
            nc.sync.dma_start(out=res[g, t][:, lo:hi], in_=r[g, t * P : (t + 1) * P, lo:hi])

        def store(g, t):
            nc.sync.dma_start(out=out[g, t * P : (t + 1) * P, :], in_=y[g, t][:])

        def views(lo, hi):
            h, at = divmod(lo, N_TILE)
            dst = grouped[h][:, at : at + hi - lo, :].rearrange("p (c i) (a e) -> p c a e i", i=4, e=2)
            src = rows_of[h][:, :, :, at : at + hi - lo].rearrange("p a e (c i) -> p c a e i", i=4)
            return dst, src

        def interleave_vector(lo, hi):
            dst, src = views(lo, hi)
            nc.vector.tensor_copy(out=dst, in_=src)

        def interleave_scalar(lo, hi):
            dst, src = views(lo, hi)
            nc.scalar.copy(out=dst, in_=src)

        def quantize(lo, hi):
            h, at = divmod(lo, N_TILE)
            part = slice(at, at + hi - lo)
            nc.vector.quantize_mx(
                out=codes[h][:, part].bitcast(FP8X4),
                scales=scales[h][:, part],
                in_=grouped[h][:, part, :].rearrange("p c j -> p (c j)"),
            )

        def multiply(g, t, h):
            rows = slice(g * ROWS, (g + 1) * ROWS)
            nc.tensor.matmul_mx(
                out=acc[g, t, h][:],
                lhsT=w_sb[rows, 2 * t * M_TILE : 2 * (t + 1) * M_TILE].bitcast(FP4X4),
                lhsT_scale=ws_sb[rows, t * M_TILE : (t + 1) * M_TILE],
                rhs=codes[h][rows, :].bitcast(FP8X4),
                rhs_scale=scales[h][rows, :],
                start=True,
                stop=True,
            )

        def relu(g, t, h):
            k = g * M_TILES + t
            nc.scalar.activation(out=y[g, t][:, cols(h)], in_=acc[g, t, h][:], func=ACT.Relu, bias=bias[:, 32 * k : 32 * k + 1])

        def add(g, t, h):
            nc.vector.tensor_tensor(out=y[g, t][:, cols(h)], in0=y[g, t][:, cols(h)], in1=res[g, t][:, cols(h)], op=ALU.add)

        nc.vector.memset(ws_sb[:].bitcast(I32), 0)
        nc.vector.memset(bias_rows[:], 0.0)
        load_weights()
        load_x_early()
        load_scales()
        load_bias()
        load_x_late()
        load_res(0, 0, 0, N)
        load_res(1, 0, 0, N_TILE)
        load_res(0, 1, 0, N)
        load_res(1, 1, 0, N)
        load_res(1, 0, N_TILE, N)

        for h in range(HALVES):
            lo = h * N_TILE
            interleave_scalar(lo + N_TILE - SCALAR_COLS[h], lo + N_TILE)
            interleave_vector(lo, lo + 256)
            interleave_vector(lo + 256, lo + N_TILE - SCALAR_COLS[h])
            quantize(lo, lo + 256)
            quantize(lo + 256, lo + 512)
            if h == 0:
                nc.vector.transpose(out=bias[:], in_=bias_rows[:])
        for g, t, h in ((0, 0, 0), (1, 0, 0), (0, 1, 0), (0, 0, 1), (1, 1, 0), (0, 1, 1), (1, 1, 1), (1, 0, 1)):
            multiply(g, t, h)

        for g, t, h in ((0, 0, 0), (1, 0, 0), (0, 1, 0), (0, 0, 1), (1, 1, 0), (0, 1, 1), (1, 1, 1), (1, 0, 1)):
            relu(g, t, h)
            add(g, t, h)
            nc.sync.dma_start(out=out[g, t * P : (t + 1) * P, cols(h)], in_=y[g, t][:, cols(h)])
